import numpy as np, ml_dtypes
CORES = [13,21,141,149]
N = 4
NB, TK, FT = 16, 128, 1
def setup_inputs(rng):
    return {"x": rng.standard_normal((N, NB, 128, TK), dtype=np.float32).astype(ml_dtypes.bfloat16), "w1": (rng.standard_normal((N, 128, FT * 128), dtype=np.float32) / 8).astype(ml_dtypes.bfloat16), "w2": (rng.standard_normal((N, 128, FT * 128), dtype=np.float32) / np.float32(8 * np.sqrt(FT))).astype(ml_dtypes.bfloat16)}
def setup_inputs_big(rng):
    d = setup_inputs(rng)
    for k in ("x",): d[k] = (d[k].astype(np.float32) * 1048576.0).astype(d[k].dtype)
    return d
def setup_inputs_small(rng):
    d = setup_inputs(rng)
    for k in ("x",): d[k] = (d[k].astype(np.float32) * (1 / 1048576.0)).astype(d[k].dtype)
    return d
def reference(x, w1, w2):
    W1, W2 = w1.astype(np.float64), w2.astype(np.float64)
    a = x[0].astype(np.float64)
    for s in range(N):
        a = sum(np.einsum("kf,bkn->bfn", W2[s][:, 128 * f:128 * f + 128], np.maximum(np.einsum("kf,bkn->bfn", W1[s][:, 128 * f:128 * f + 128], a), 0.0)) for f in range(FT))
    y = np.full(x.shape, np.nan, ml_dtypes.bfloat16)
    y[N - 1] = a.astype(ml_dtypes.bfloat16)
    return {"y": y}

@@ -1,0 +1,232 @@
+from concourse.bass import DstId, RemoteDMATransfer
+from concourse.mybir import AluOpType
+
+NB, TK = 16, 128
+NSIM = 256
+PAIRS = [2, 2, 4, 4, 4]
+UNITS = []
+_b = 0
+for _p in PAIRS:
+    UNITS.append((_b, _p // 2))
+    UNITS.append((_b + _p // 2, _p // 2))
+    _b += _p
+NU = len(UNITS)
+PREP = ["T1", "T0", "C0", "C1", "T2", "C2"]
+
+SCRATCH = {
+    "w": ("sbuf", [128, 256], "bfloat16"),
+    "xin": ("sbuf", [128, NB * TK], "bfloat16"),
+    "h": ("sbuf", [128, NB * TK], "bfloat16"),
+    "zero": ("sbuf", [128, 512], "float32"),
+    "w0r": ("sbuf", [128, 128], "bfloat16"),
+    "w1r": ("sbuf", [128, 256], "bfloat16"),
+    "w2r": ("sbuf", [128, 256], "bfloat16"),
+    "idz": ("sbuf", [128, 129], "bfloat16"),
+    "idd": ("dram", [129, 128], "bfloat16"),
+    "ident": ("sbuf", [128, 128], "bfloat16"),
+    "wt": ("sbuf", [128, 384], "bfloat16"),
+    "cc": ("sbuf", [128, 384], "bfloat16"),
+    "a1": ("sbuf", [128, NB * TK], "bfloat16"),
+    "a2": ("sbuf", [128, NB * TK], "bfloat16"),
+    "a3": ("sbuf", [128, NB * TK], "bfloat16"),
+    "yo": ("sbuf", [128, NB * TK], "bfloat16"),
+    "ps": ("psum", [128, 4096], "float32"),
+}
+SEMAPHORES = (["lw1", "lw2", "zs", "ids", "id1", "id2", "snt", "ws", "wa1", "wa2", "st", "pm0", "pm1", "pv0", "pv1"]
+              + ["xs%d" % u for u in range(NU)] + ["m%d" % u for u in range(NU)] + ["v%d" % u for u in range(NU)]
+              + ["ha%d" % u for u in range(NU)] + ["p" + n for n in PREP] + ["q" + n for n in PREP])
+
+
+def _engines(topo, src, dst):
+    m = topo.mask(src, dst)
+    return [e for e in range(m.bit_length()) if (m >> e) & 1]
+
+
+def _bits(es):
+    return sum(1 << e for e in es)
+
+
+def _chip_cores(topo, c):
+    return [d for d in range(NSIM) if topo.host(d) == topo.host(c) and topo.chip(d) == topo.chip(c) and d != c]
+
+
+def _owners(topo, c, dst):
+    own = [d for d in _chip_cores(topo, c) if topo.may_write(d, dst)]
+    near = [d for d in own if topo.die(d) == topo.die(c)]
+    far = [d for d in own if topo.die(d) != topo.die(c)]
+    out = []
+    for i in range(max(len(near), len(far))):
+        out += near[i:i + 1] + far[i:i + 1]
+    return out
+
+
+def _cols(u):
+    b, n = UNITS[u]
+    return b * TK, (b + n) * TK
+
+
+def rank_program(g, core, T, topo):
+    S = T.sem
+    r0, r1, r2, r3 = T.cores
+    XR = _owners(topo, r0, r3)[:4]
+    WR = _owners(topo, r2, r3)[0]
+    NR = len(XR)
+    SW = 128 // NR
+    te, ve = g.tensor, g.vector
+
+    def send(dst, out_ap, in_ap, sem, es):
+        rid, pid = topo.addr(dst, core)
+        g.remote_dma(out_ap=out_ap, in_ap=in_ap, remote_sem=sem, local_sem=S.snt, pid=pid, routing_id=rid,
+                     dma_engine_mask=_bits(es))
+        return len(es)
+
+    def load_w():
+        g.sync.dma_start(T.w[:, 0:128], T.w1[:, :]).then_inc(S.lw1, 16)
+        g.scalar.dma_start(T.w[:, 128:256], T.w2[:, :]).then_inc(S.lw2, 16)
+
+    if core == r0:
+        load_w()
+        for u in range(NU):
+            b0, n = UNITS[u]
+            for b in range(b0, b0 + n):
+                q = g.sync if b % 2 == 0 else g.scalar
+                q.dma_start(T.xin[:, b * TK:(b + 1) * TK], T.x[b]).then_inc(S["xs%d" % u], 16)
+        ve.memset(T.zero[:, :], 0.0).then_inc(S.zs, 1)
+        ve.wait_ge(S.zs, 1)
+        te.wait_ge(S.lw1, 16)
+        for u in range(NU):
+            c0, c1 = _cols(u)
+            n = c1 - c0
+            bk = T.ps[:, (u % 8) * 512:(u % 8) * 512 + n]
+            te.wait_ge(S["xs%d" % u], 16 * UNITS[u][1])
+            if u >= 8:
+                te.wait_ge(S["v%d" % (u - 8)], 1)
+            te.matmul(bk, T.w[:, 0:128], T.xin[:, c0:c1], True, True).then_inc(S["m%d" % u], 1)
+            ve.wait_ge(S["m%d" % u], 1)
+            ve.tensor_tensor(T.h[:, c0:c1], bk, T.zero[:, 0:n], AluOpType.max).then_inc(S["v%d" % u], 1)
+        es = _engines(topo, core, XR[0])[:8]
+        sent = 0
+        k = len(es) // NR
+        g.wait_ge(S.lw2, 16)
+        trs = []
+        for j, d in enumerate(XR):
+            rid, pid = topo.addr(d, core)
+            trs.append(RemoteDMATransfer(dst_ids=[DstId(rid=rid, pnc=pid)], dma_engine_mask=_bits(es[j * k:(j + 1) * k]),
+                                         remote_sem=S.ws, src=T.w[:, 128 + j * SW:128 + (j + 1) * SW],
+                                         dst=T.w0r[:, j * SW:(j + 1) * SW]))
+            sent += k
+        g.remote_dma_fused(trs, local_sem=S.snt)
+        k = len(es) // 2
+        for p in range(NU // 2):
+            trs = []
+            for i in range(2):
+                u = 2 * p + i
+                c0, c1 = _cols(u)
+                g.wait_ge(S["v%d" % u], 1)
+                rid, pid = topo.addr(XR[u % NR], core)
+                trs.append(RemoteDMATransfer(dst_ids=[DstId(rid=rid, pnc=pid)], dma_engine_mask=_bits(es[i * k:(i + 1) * k]),
+                                             remote_sem=S["ha%d" % u], src=T.h[:, c0:c1], dst=T.h[:, c0:c1]))
+                sent += k
+            g.remote_dma_fused(trs, local_sem=S.snt)
+        g.wait_ge(S.snt, sent)
+        return
+
+    if core in XR:
+        j = XR.index(core)
+        n_on = len(_engines(topo, r0, XR[0])[:8])
+        es = _engines(topo, core, r3)
+        g.wait_ge(S.ws, n_on // NR)
+        sent = send(r3, T.w0r[:, j * SW:(j + 1) * SW], T.w0r[:, j * SW:(j + 1) * SW], S.ws, es)
+        for u in range(NU):
+            if u % NR != j:
+                continue
+            c0, c1 = _cols(u)
+            g.wait_ge(S["ha%d" % u], n_on // 2)
+            sent += send(r3, T.h[:, c0:c1], T.h[:, c0:c1], S["ha%d" % u], es)
+        g.wait_ge(S.snt, sent)
+        return
+
+    if core == r1:
+        load_w()
+        g.wait_ge(S.lw1, 16)
+        g.wait_ge(S.lw2, 16)
+        sent = send(r3, T.w1r[:, :], T.w[:, :], S.wa1, _engines(topo, core, r3))
+        g.wait_ge(S.snt, sent)
+        return
+
+    if core == r2:
+        load_w()
+        g.wait_ge(S.lw1, 16)
+        g.wait_ge(S.lw2, 16)
+        sent = send(WR, T.w2r[:, :], T.w[:, :], S.wa2, _engines(topo, core, WR)[:8])
+        g.wait_ge(S.snt, sent)
+        return
+    if core == WR:
+        g.wait_ge(S.wa2, len(_engines(topo, r2, WR)[:8]))
+        sent = send(r3, T.w2r[:, :], T.w2r[:, :], S.wa2, _engines(topo, core, r3))
+        g.wait_ge(S.snt, sent)
+        return
+
+    if core != r3:
+        return
+
+    n_off = len(_engines(topo, XR[0], r3))
+    ve.memset(T.idz[:, :], 0.0).then_inc(S.ids, 1)
+    ve.wait_ge(S.ids, 1)
+    ve.memset(T.idz[:, 0:1], 1.0).then_inc(S.ids, 1)
+    ve.memset(T.zero[:, :], 0.0).then_inc(S.zs, 1)
+    ve.wait_ge(S.zs, 1)
+    g.sync.wait_ge(S.ids, 2)
+    g.sync.dma_start(T.idd[:, :], T.idz[:, :]).then_inc(S.id1, 16)
+    g.sync.wait_ge(S.id1, 16)
+    g.sync.dma_start(T.ident[:, :], T.idd[0:128, :]).then_inc(S.id2, 16)
+    g.scalar.dma_start(T.w[:, 0:128], T.w1[:, :]).then_inc(S.lw1, 16)
+    g.scalar.dma_start(T.w[:, 128:256], T.w2[:, :]).then_inc(S.lw2, 16)
+
+    def prep(name, lhsT, rhs, out, waits):
+        bk = T.ps[:, (2 + PREP.index(name)) * 512:(2 + PREP.index(name)) * 512 + 128]
+        for s, v in waits:
+            te.wait_ge(s, v)
+        te.matmul(bk, lhsT, rhs, True, True).then_inc(S["p" + name], 1)
+        ve.wait_ge(S["p" + name], 1)
+        ve.tensor_copy(out, bk).then_inc(S["q" + name], 1)
+
+    prep("T1", T.w1r[:, 128:256], T.ident[:, :], T.wt[:, 128:256], [(S.id2, 16), (S.wa1, len(_engines(topo, r1, r3)))])
+    prep("T0", T.w0r[:, :], T.ident[:, :], T.wt[:, 0:128], [(S.ws, NR * n_off)])
+    prep("C0", T.wt[:, 0:128], T.w1r[:, 0:128], T.cc[:, 0:128], [(S.qT0, 1)])
+    prep("C1", T.wt[:, 128:256], T.w2r[:, 0:128], T.cc[:, 128:256], [(S.wa2, len(_engines(topo, WR, r3))), (S.qT1, 1)])
+    prep("T2", T.w2r[:, 128:256], T.ident[:, :], T.wt[:, 256:384], [])
+
+    cnt = [0, 0]
+    pm, pv = [S.pm0, S.pm1], [S.pv0, S.pv1]
+    lhs = [T.cc[:, 0:128], T.cc[:, 128:256], T.cc[:, 256:384], T.w[:, 128:256]]
+    act = [T.h, T.a1, T.a2, T.a3, T.yo]
+    ready = [(S.qC0, 1), (S.qC1, 1), (S.qC2, 1), (S.lw2, 16)]
+    for p in range(NU // 2):
+        for s in range(4):
+            if p == 0:
+                te.wait_ge(ready[s][0], ready[s][1])
+            for i in range(2):
+                u = 2 * p + i
+                c0, c1 = _cols(u)
+                n = c1 - c0
+                bk = T.ps[:, i * 512:i * 512 + n]
+                if s == 0:
+                    te.wait_ge(S["ha%d" % u], n_off)
+                if cnt[i]:
+                    te.wait_ge(pv[i], cnt[i])
+                te.matmul(bk, lhs[s], act[s][:, c0:c1], True, True).then_inc(pm[i], 1)
+                cnt[i] += 1
+                ve.wait_ge(pm[i], cnt[i])
+                if s < 3:
+                    ve.tensor_tensor(act[s + 1][:, c0:c1], bk, T.zero[:, 0:n], AluOpType.max).then_inc(pv[i], 1)
+                else:
+                    ve.tensor_copy(T.yo[:, c0:c1], bk).then_inc(pv[i], 1)
+                    b0, nb = UNITS[u]
+                    for b in range(b0, b0 + nb):
+                        q = g.sync if b % 2 == 0 else g.scalar
+                        q.wait_ge(pv[i], cnt[i])
+                        q.dma_start(T.y[b], T.yo[:, b * TK:(b + 1) * TK]).then_inc(S.st, 16)
+            if p == 0 and s == 0:
+                prep("C2", T.wt[:, 256:384], T.w[:, 0:128], T.cc[:, 256:384], [(S.qT2, 1), (S.lw1, 16)])
+    g.wait_ge(S.st, 16 * NB)

@@ -3,38 +3,44 @@ from concourse.mybir import AluOpType
 
 NB, TK = 16, 128
 NSIM = 256
-PAIRS = [2, 2, 4, 4, 4]
+PAIRS = [2, 2, 4]
 UNITS = []
 _b = 0
 for _p in PAIRS:
     UNITS.append((_b, _p // 2))
     UNITS.append((_b + _p // 2, _p // 2))
     _b += _p
+ND = len(UNITS)
+NBD = _b
+for _j in range(4):
+    UNITS.append((_b, 2))
+    _b += 2
 NU = len(UNITS)
 PREP = ["T1", "T0", "C0", "C1", "T2", "C2"]
+_ACT = ("sbuf", [128, NB * TK], "bfloat16")
 
 SCRATCH = {
     "w": ("sbuf", [128, 256], "bfloat16"),
-    "xin": ("sbuf", [128, NB * TK], "bfloat16"),
-    "h": ("sbuf", [128, NB * TK], "bfloat16"),
+    "xin": _ACT,
+    "h": _ACT,
     "zero": ("sbuf", [128, 512], "float32"),
     "w0r": ("sbuf", [128, 128], "bfloat16"),
     "w1r": ("sbuf", [128, 256], "bfloat16"),
     "w2r": ("sbuf", [128, 256], "bfloat16"),
+    "w3r": ("sbuf", [128, 256], "bfloat16"),
     "idz": ("sbuf", [128, 129], "bfloat16"),
     "idd": ("dram", [129, 128], "bfloat16"),
     "ident": ("sbuf", [128, 128], "bfloat16"),
     "wt": ("sbuf", [128, 384], "bfloat16"),
     "cc": ("sbuf", [128, 384], "bfloat16"),
-    "a1": ("sbuf", [128, NB * TK], "bfloat16"),
-    "a2": ("sbuf", [128, NB * TK], "bfloat16"),
-    "a3": ("sbuf", [128, NB * TK], "bfloat16"),
-    "yo": ("sbuf", [128, NB * TK], "bfloat16"),
+    "a1": _ACT, "a2": _ACT, "a3": _ACT, "a4": _ACT, "a5": _ACT, "a6": _ACT, "yo": _ACT,
+    "yd": ("dram", [NB - NBD, 128, TK], "bfloat16"),
     "ps": ("psum", [128, 4096], "float32"),
 }
-SEMAPHORES = (["lw1", "lw2", "zs", "ids", "id1", "id2", "snt", "ws", "wa1", "wa2", "st", "pm0", "pm1", "pv0", "pv1"]
+SEMAPHORES = (["lw1", "lw2", "zs", "ids", "id1", "id2", "snt", "ws", "wa1", "wa2", "wa3", "st", "pm0", "pm1", "pv0", "pv1"]
               + ["xs%d" % u for u in range(NU)] + ["m%d" % u for u in range(NU)] + ["v%d" % u for u in range(NU)]
-              + ["ha%d" % u for u in range(NU)] + ["p" + n for n in PREP] + ["q" + n for n in PREP])
+              + ["ha%d" % u for u in range(NU)] + ["yk%d" % j for j in range(4)]
+              + ["p" + n for n in PREP] + ["q" + n for n in PREP])
 
 
 def _engines(topo, src, dst):
@@ -70,6 +76,8 @@ def rank_program(g, core, T, topo):
     r0, r1, r2, r3 = T.cores
     XR = _owners(topo, r0, r3)[:4]
     WR = _owners(topo, r2, r3)[0]
+    E1 = _owners(topo, r1, XR[0])[:2]
+    E3 = _owners(topo, r3, XR[0])[:2]
     NR = len(XR)
     SW = 128 // NR
     te, ve = g.tensor, g.vector
@@ -80,12 +88,24 @@ def rank_program(g, core, T, topo):
                      dma_engine_mask=_bits(es))
         return len(es)
 
-    def load_w():
-        g.sync.dma_start(T.w[:, 0:128], T.w1[:, :]).then_inc(S.lw1, 16)
-        g.scalar.dma_start(T.w[:, 128:256], T.w2[:, :]).then_inc(S.lw2, 16)
+    def fused(items, es):
+        k = len(es) // len(items)
+        trs = []
+        for i, (d, out_ap, in_ap, sem) in enumerate(items):
+            rid, pid = topo.addr(d, core)
+            trs.append(RemoteDMATransfer(dst_ids=[DstId(rid=rid, pnc=pid)], dma_engine_mask=_bits(es[i * k:(i + 1) * k]),
+                                         remote_sem=sem, src=in_ap, dst=out_ap))
+        g.remote_dma_fused(trs, local_sem=S.snt)
+        return k * len(items)
+
+    def load_w(qa, qb):
+        qa.dma_start(T.w[:, 0:128], T.w1[:, :]).then_inc(S.lw1, 16)
+        qb.dma_start(T.w[:, 128:256], T.w2[:, :]).then_inc(S.lw2, 16)
+
+    on8 = 8
 
     if core == r0:
-        load_w()
+        load_w(g.sync, g.scalar)
         for u in range(NU):
             b0, n = UNITS[u]
             for b in range(b0, b0 + n):
@@ -104,65 +124,96 @@ def rank_program(g, core, T, topo):
             te.matmul(bk, T.w[:, 0:128], T.xin[:, c0:c1], True, True).then_inc(S["m%d" % u], 1)
             ve.wait_ge(S["m%d" % u], 1)
             ve.tensor_tensor(T.h[:, c0:c1], bk, T.zero[:, 0:n], AluOpType.max).then_inc(S["v%d" % u], 1)
-        es = _engines(topo, core, XR[0])[:8]
-        sent = 0
-        k = len(es) // NR
+        full = _engines(topo, core, XR[0])
+        es = full[:on8]
         g.wait_ge(S.lw2, 16)
-        trs = []
-        for j, d in enumerate(XR):
-            rid, pid = topo.addr(d, core)
-            trs.append(RemoteDMATransfer(dst_ids=[DstId(rid=rid, pnc=pid)], dma_engine_mask=_bits(es[j * k:(j + 1) * k]),
-                                         remote_sem=S.ws, src=T.w[:, 128 + j * SW:128 + (j + 1) * SW],
-                                         dst=T.w0r[:, j * SW:(j + 1) * SW]))
-            sent += k
-        g.remote_dma_fused(trs, local_sem=S.snt)
-        k = len(es) // 2
-        for p in range(NU // 2):
-            trs = []
-            for i in range(2):
-                u = 2 * p + i
+        sent = fused([(d, T.w0r[:, :], T.w[:, 128:256], S.ws) for d in XR], es)
+        for p in range(ND // 2):
+            items = []
+            for u in (2 * p, 2 * p + 1):
                 c0, c1 = _cols(u)
                 g.wait_ge(S["v%d" % u], 1)
-                rid, pid = topo.addr(XR[u % NR], core)
-                trs.append(RemoteDMATransfer(dst_ids=[DstId(rid=rid, pnc=pid)], dma_engine_mask=_bits(es[i * k:(i + 1) * k]),
-                                             remote_sem=S["ha%d" % u], src=T.h[:, c0:c1], dst=T.h[:, c0:c1]))
-                sent += k
-            g.remote_dma_fused(trs, local_sem=S.snt)
+                items.append((XR[u % NR], T.h[:, c0:c1], T.h[:, c0:c1], S["ha%d" % u]))
+            sent += fused(items, es)
+        items = []
+        for j in range(NR):
+            u = ND + j
+            c0, c1 = _cols(u)
+            g.wait_ge(S["v%d" % u], 1)
+            items.append((XR[j], T.h[:, c0:c1], T.h[:, c0:c1], S["ha%d" % u]))
+        sent += fused(items, full)
         g.wait_ge(S.snt, sent)
         return
 
     if core in XR:
         j = XR.index(core)
-        n_on = len(_engines(topo, r0, XR[0])[:8])
         es = _engines(topo, core, r3)
-        g.wait_ge(S.ws, n_on // NR)
+        n_full = len(_engines(topo, r0, XR[0]))
+        n_e = len(_engines(topo, E1[0], core)) // 2
+        g.wait_ge(S.ws, on8 // NR)
         sent = send(r3, T.w0r[:, j * SW:(j + 1) * SW], T.w0r[:, j * SW:(j + 1) * SW], S.ws, es)
-        for u in range(NU):
+        for u in range(ND):
             if u % NR != j:
                 continue
             c0, c1 = _cols(u)
-            g.wait_ge(S["ha%d" % u], n_on // 2)
+            g.wait_ge(S["ha%d" % u], on8 // 2)
             sent += send(r3, T.h[:, c0:c1], T.h[:, c0:c1], S["ha%d" % u], es)
+        ve.memset(T.zero[:, :], 0.0).then_inc(S.zs, 1)
+        ve.wait_ge(S.zs, 1)
+        b0 = UNITS[ND + j][0]
+        tiles = [(T.w0r[:, :], (S.ws, on8 // NR)), (T.w1r[:, 0:128], (S.wa1, n_e)), (T.w1r[:, 128:256], None),
+                 (T.w2r[:, 0:128], (S.wa2, len(es) // NR)), (T.w2r[:, 128:256], None),
+                 (T.w3r[:, 0:128], (S.wa3, n_e)), (T.w3r[:, 128:256], None)]
+        bufs = [T.h, T.a1, T.a2, T.a3, T.a4, T.a5, T.a6, T.yo]
+        pm, pv = [S.pm0, S.pm1], [S.pv0, S.pv1]
+        te.wait_ge(S["ha%d" % (ND + j)], n_full // NR)
+        for s, (tile, wt) in enumerate(tiles):
+            if wt is not None:
+                te.wait_ge(wt[0], wt[1])
+            for i in range(2):
+                c0 = (b0 + i) * TK
+                bk = T.ps[:, i * 512:i * 512 + TK]
+                if s:
+                    te.wait_ge(pv[i], s)
+                te.matmul(bk, tile, bufs[s][:, c0:c0 + TK], True, True).then_inc(pm[i], 1)
+                ve.wait_ge(pm[i], s + 1)
+                if s % 2 == 1:
+                    ve.tensor_tensor(bufs[s + 1][:, c0:c0 + TK], bk, T.zero[:, 0:TK], AluOpType.max).then_inc(pv[i], 1)
+                else:
+                    ve.tensor_copy(bufs[s + 1][:, c0:c0 + TK], bk).then_inc(pv[i], 1)
+        g.wait_ge(S.pv0, len(tiles))
+        g.wait_ge(S.pv1, len(tiles))
+        sent += fused([(r3, T.yd[b0 + i - NBD], T.yo[:, (b0 + i) * TK:(b0 + i + 1) * TK], S["yk%d" % j]) for i in range(2)], es)
         g.wait_ge(S.snt, sent)
         return
 
     if core == r1:
-        load_w()
+        load_w(g.sync, g.scalar)
         g.wait_ge(S.lw1, 16)
         g.wait_ge(S.lw2, 16)
-        sent = send(r3, T.w1r[:, :], T.w[:, :], S.wa1, _engines(topo, core, r3))
+        sent = fused([(d, T.w1r[:, :], T.w[:, :], S.wa1) for d in E1], _engines(topo, core, E1[0])[:on8])
+        sent += send(r3, T.w1r[:, :], T.w[:, :], S.wa1, _engines(topo, core, r3))
         g.wait_ge(S.snt, sent)
         return
 
+    for ee, buf, sem in ((E1, T.w1r, S.wa1), (E3, T.w3r, S.wa3)):
+        if core in ee:
+            g.wait_ge(sem, on8 // 2)
+            mine = [d for d in XR if topo.die(d) == topo.die(core)]
+            sent = fused([(d, buf[:, :], buf[:, :], sem) for d in mine], _engines(topo, core, mine[0]))
+            g.wait_ge(S.snt, sent)
+            return
+
     if core == r2:
-        load_w()
+        load_w(g.sync, g.scalar)
         g.wait_ge(S.lw1, 16)
         g.wait_ge(S.lw2, 16)
-        sent = send(WR, T.w2r[:, :], T.w[:, :], S.wa2, _engines(topo, core, WR)[:8])
+        sent = send(WR, T.w2r[:, :], T.w[:, :], S.wa2, _engines(topo, core, WR)[:on8])
+        sent += fused([(d, T.w2r[:, :], T.w[:, :], S.wa2) for d in XR], _engines(topo, core, XR[0]))
         g.wait_ge(S.snt, sent)
         return
     if core == WR:
-        g.wait_ge(S.wa2, len(_engines(topo, r2, WR)[:8]))
+        g.wait_ge(S.wa2, on8)
         sent = send(r3, T.w2r[:, :], T.w2r[:, :], S.wa2, _engines(topo, core, r3))
         g.wait_ge(S.snt, sent)
         return
@@ -171,6 +222,10 @@ def rank_program(g, core, T, topo):
         return
 
     n_off = len(_engines(topo, XR[0], r3))
+    load_w(g.scalar, g.scalar)
+    g.wait_ge(S.lw1, 16)
+    g.wait_ge(S.lw2, 16)
+    sent = fused([(d, T.w3r[:, :], T.w[:, :], S.wa3) for d in E3], _engines(topo, core, E3[0])[:on8])
     ve.memset(T.idz[:, :], 0.0).then_inc(S.ids, 1)
     ve.wait_ge(S.ids, 1)
     ve.memset(T.idz[:, 0:1], 1.0).then_inc(S.ids, 1)
@@ -180,8 +235,6 @@ def rank_program(g, core, T, topo):
     g.sync.dma_start(T.idd[:, :], T.idz[:, :]).then_inc(S.id1, 16)
     g.sync.wait_ge(S.id1, 16)
     g.sync.dma_start(T.ident[:, :], T.idd[0:128, :]).then_inc(S.id2, 16)
-    g.scalar.dma_start(T.w[:, 0:128], T.w1[:, :]).then_inc(S.lw1, 16)
-    g.scalar.dma_start(T.w[:, 128:256], T.w2[:, :]).then_inc(S.lw2, 16)
 
     def prep(name, lhsT, rhs, out, waits):
         bk = T.ps[:, (2 + PREP.index(name)) * 512:(2 + PREP.index(name)) * 512 + 128]
@@ -202,7 +255,7 @@ def rank_program(g, core, T, topo):
     lhs = [T.cc[:, 0:128], T.cc[:, 128:256], T.cc[:, 256:384], T.w[:, 128:256]]
     act = [T.h, T.a1, T.a2, T.a3, T.yo]
     ready = [(S.qC0, 1), (S.qC1, 1), (S.qC2, 1), (S.lw2, 16)]
-    for p in range(NU // 2):
+    for p in range(ND // 2):
         for s in range(4):
             if p == 0:
                 te.wait_ge(ready[s][0], ready[s][1])
@@ -223,10 +276,14 @@ def rank_program(g, core, T, topo):
                 else:
                     ve.tensor_copy(T.yo[:, c0:c1], bk).then_inc(pv[i], 1)
                     b0, nb = UNITS[u]
+                    g.sync.wait_ge(pv[i], cnt[i])
                     for b in range(b0, b0 + nb):
-                        q = g.sync if b % 2 == 0 else g.scalar
-                        q.wait_ge(pv[i], cnt[i])
-                        q.dma_start(T.y[b], T.yo[:, b * TK:(b + 1) * TK]).then_inc(S.st, 16)
+                        g.sync.dma_start(T.y[b], T.yo[:, b * TK:(b + 1) * TK]).then_inc(S.st, 16)
             if p == 0 and s == 0:
                 prep("C2", T.wt[:, 256:384], T.w[:, 0:128], T.cc[:, 256:384], [(S.qT2, 1), (S.lw1, 16)])
-    g.wait_ge(S.st, 16 * NB)
+    for j in range(NR):
+        b0 = UNITS[ND + j][0]
+        g.scalar.wait_ge(S["yk%d" % j], n_off)
+        g.scalar.dma_start(T.y[b0:b0 + 2], T.yd[b0 - NBD:b0 - NBD + 2]).then_inc(S.st, 16)
+    g.wait_ge(S.snt, sent)
+    g.wait_ge(S.st, 16 * (NBD + NR))

@@ -3,7 +3,8 @@ from concourse.mybir import AluOpType
 
 NB, TK = 16, 128
 NSIM = 256
-PAIRS = [2, 2, 4]
+RB = 2
+PAIRS = [2, 6]
 UNITS = []
 _b = 0
 for _p in PAIRS:
@@ -13,8 +14,8 @@ for _p in PAIRS:
 ND = len(UNITS)
 NBD = _b
 for _j in range(4):
-    UNITS.append((_b, 2))
-    _b += 2
+    UNITS.append((_b, RB))
+    _b += RB
 NU = len(UNITS)
 PREP = ["T1", "T0", "C0", "C1", "T2", "C2"]
 _ACT = ("sbuf", [128, NB * TK], "bfloat16")
@@ -37,7 +38,8 @@ SCRATCH = {
     "yd": ("dram", [NB - NBD, 128, TK], "bfloat16"),
     "ps": ("psum", [128, 4096], "float32"),
 }
-SEMAPHORES = (["lw1", "lw2", "zs", "ids", "id1", "id2", "snt", "ws", "wa1", "wa2", "wa3", "st", "pm0", "pm1", "pv0", "pv1"]
+SEMAPHORES = (["lw1", "lw2", "zs", "ids", "id1", "id2", "snt", "ws", "wa1", "wa2", "wa3", "st"]
+              + ["pm%d" % i for i in range(4)] + ["pv%d" % i for i in range(4)]
               + ["xs%d" % u for u in range(NU)] + ["m%d" % u for u in range(NU)] + ["v%d" % u for u in range(NU)]
               + ["ha%d" % u for u in range(NU)] + ["yk%d" % j for j in range(4)]
               + ["p" + n for n in PREP] + ["q" + n for n in PREP])
@@ -52,18 +54,18 @@ def _bits(es):
     return sum(1 << e for e in es)
 
 
-def _chip_cores(topo, c):
-    return [d for d in range(NSIM) if topo.host(d) == topo.host(c) and topo.chip(d) == topo.chip(c) and d != c]
-
-
-def _owners(topo, c, dst):
-    own = [d for d in _chip_cores(topo, c) if topo.may_write(d, dst)]
-    near = [d for d in own if topo.die(d) == topo.die(c)]
-    far = [d for d in own if topo.die(d) != topo.die(c)]
+def _turns(topo, cores, c):
+    near = [d for d in cores if topo.die(d) == topo.die(c)]
+    far = [d for d in cores if topo.die(d) != topo.die(c)]
     out = []
     for i in range(max(len(near), len(far))):
         out += near[i:i + 1] + far[i:i + 1]
     return out
+
+
+def _owners(topo, c, dst):
+    chip = [d for d in range(NSIM) if topo.host(d) == topo.host(c) and topo.chip(d) == topo.chip(c) and d != c]
+    return _turns(topo, [d for d in chip if topo.may_write(d, dst)], c)
 
 
 def _cols(u):
@@ -75,9 +77,10 @@ def rank_program(g, core, T, topo):
     S = T.sem
     r0, r1, r2, r3 = T.cores
     XR = _owners(topo, r0, r3)[:4]
-    WR = _owners(topo, r2, r3)[0]
+    WR, V2 = _owners(topo, r2, r3)[:2]
     E1 = _owners(topo, r1, XR[0])[:2]
-    E3 = _owners(topo, r3, XR[0])[:2]
+    E3 = _turns(topo, [c for c in range(NSIM) if topo.mates(c, XR[0]) and topo.may_write(c, XR[0])
+                       and topo.may_write(r3, c)], r3)[:2]
     NR = len(XR)
     SW = 128 // NR
     te, ve = g.tensor, g.vector
@@ -101,6 +104,9 @@ def rank_program(g, core, T, topo):
     def load_w(qa, qb):
         qa.dma_start(T.w[:, 0:128], T.w1[:, :]).then_inc(S.lw1, 16)
         qb.dma_start(T.w[:, 128:256], T.w2[:, :]).then_inc(S.lw2, 16)
+
+    def same_die(c):
+        return [d for d in XR if topo.die(d) == topo.die(c)]
 
     on8 = 8
 
@@ -149,7 +155,7 @@ def rank_program(g, core, T, topo):
         j = XR.index(core)
         es = _engines(topo, core, r3)
         n_full = len(_engines(topo, r0, XR[0]))
-        n_e = len(_engines(topo, E1[0], core)) // 2
+        n_e = len(es) // 2
         g.wait_ge(S.ws, on8 // NR)
         sent = send(r3, T.w0r[:, j * SW:(j + 1) * SW], T.w0r[:, j * SW:(j + 1) * SW], S.ws, es)
         for u in range(ND):
@@ -162,28 +168,29 @@ def rank_program(g, core, T, topo):
         ve.wait_ge(S.zs, 1)
         b0 = UNITS[ND + j][0]
         tiles = [(T.w0r[:, :], (S.ws, on8 // NR)), (T.w1r[:, 0:128], (S.wa1, n_e)), (T.w1r[:, 128:256], None),
-                 (T.w2r[:, 0:128], (S.wa2, len(es) // NR)), (T.w2r[:, 128:256], None),
+                 (T.w2r[:, 0:128], (S.wa2, n_e)), (T.w2r[:, 128:256], None),
                  (T.w3r[:, 0:128], (S.wa3, n_e)), (T.w3r[:, 128:256], None)]
         bufs = [T.h, T.a1, T.a2, T.a3, T.a4, T.a5, T.a6, T.yo]
-        pm, pv = [S.pm0, S.pm1], [S.pv0, S.pv1]
+        NT = len(tiles)
         te.wait_ge(S["ha%d" % (ND + j)], n_full // NR)
         for s, (tile, wt) in enumerate(tiles):
             if wt is not None:
                 te.wait_ge(wt[0], wt[1])
-            for i in range(2):
+            for i in range(RB):
+                pm, pv = S["pm%d" % i], S["pv%d" % i]
                 c0 = (b0 + i) * TK
                 bk = T.ps[:, i * 512:i * 512 + TK]
                 if s:
-                    te.wait_ge(pv[i], s)
-                te.matmul(bk, tile, bufs[s][:, c0:c0 + TK], True, True).then_inc(pm[i], 1)
-                ve.wait_ge(pm[i], s + 1)
+                    te.wait_ge(pv, s)
+                te.matmul(bk, tile, bufs[s][:, c0:c0 + TK], True, True).then_inc(pm, 1)
+                ve.wait_ge(pm, s + 1)
                 if s % 2 == 1:
-                    ve.tensor_tensor(bufs[s + 1][:, c0:c0 + TK], bk, T.zero[:, 0:TK], AluOpType.max).then_inc(pv[i], 1)
+                    ve.tensor_tensor(bufs[s + 1][:, c0:c0 + TK], bk, T.zero[:, 0:TK], AluOpType.max).then_inc(pv, 1)
                 else:
-                    ve.tensor_copy(bufs[s + 1][:, c0:c0 + TK], bk).then_inc(pv[i], 1)
-        g.wait_ge(S.pv0, len(tiles))
-        g.wait_ge(S.pv1, len(tiles))
-        sent += fused([(r3, T.yd[b0 + i - NBD], T.yo[:, (b0 + i) * TK:(b0 + i + 1) * TK], S["yk%d" % j]) for i in range(2)], es)
+                    ve.tensor_copy(bufs[s + 1][:, c0:c0 + TK], bk).then_inc(pv, 1)
+        for i in range(RB):
+            g.wait_ge(S["pv%d" % i], NT)
+        sent += fused([(r3, T.yd[b0 + i - NBD], T.yo[:, (b0 + i) * TK:(b0 + i + 1) * TK], S["yk%d" % j]) for i in range(RB)], es)
         g.wait_ge(S.snt, sent)
         return
 
@@ -196,10 +203,10 @@ def rank_program(g, core, T, topo):
         g.wait_ge(S.snt, sent)
         return
 
-    for ee, buf, sem in ((E1, T.w1r, S.wa1), (E3, T.w3r, S.wa3)):
+    for ee, buf, sem in ((E1, T.w1r, S.wa1), (E3, T.w3r, S.wa3), ([V2], T.w2r, S.wa2)):
         if core in ee:
             g.wait_ge(sem, on8 // 2)
-            mine = [d for d in XR if topo.die(d) == topo.die(core)]
+            mine = same_die(core)
             sent = fused([(d, buf[:, :], buf[:, :], sem) for d in mine], _engines(topo, core, mine[0]))
             g.wait_ge(S.snt, sent)
             return
@@ -208,12 +215,13 @@ def rank_program(g, core, T, topo):
         load_w(g.sync, g.scalar)
         g.wait_ge(S.lw1, 16)
         g.wait_ge(S.lw2, 16)
-        sent = send(WR, T.w2r[:, :], T.w[:, :], S.wa2, _engines(topo, core, WR)[:on8])
-        sent += fused([(d, T.w2r[:, :], T.w[:, :], S.wa2) for d in XR], _engines(topo, core, XR[0]))
+        sent = fused([(d, T.w2r[:, :], T.w[:, :], S.wa2) for d in (WR, V2)], _engines(topo, core, WR)[:on8])
+        mine = same_die(core)
+        sent += fused([(d, T.w2r[:, :], T.w[:, :], S.wa2) for d in mine], _engines(topo, core, mine[0]))
         g.wait_ge(S.snt, sent)
         return
     if core == WR:
-        g.wait_ge(S.wa2, on8)
+        g.wait_ge(S.wa2, on8 // 2)
         sent = send(r3, T.w2r[:, :], T.w2r[:, :], S.wa2, _engines(topo, core, r3))
         g.wait_ge(S.snt, sent)
         return
@@ -283,7 +291,7 @@ def rank_program(g, core, T, topo):
                 prep("C2", T.wt[:, 256:384], T.w[:, 0:128], T.cc[:, 256:384], [(S.qT2, 1), (S.lw1, 16)])
     for j in range(NR):
         b0 = UNITS[ND + j][0]
-        g.scalar.wait_ge(S["yk%d" % j], n_off)
-        g.scalar.dma_start(T.y[b0:b0 + 2], T.yd[b0 - NBD:b0 - NBD + 2]).then_inc(S.st, 16)
+        g.scalar.wait_ge(S["yk%d" % j], (n_off // RB) * RB)
+        g.scalar.dma_start(T.y[b0:b0 + RB], T.yd[b0 - NBD:b0 - NBD + RB]).then_inc(S.st, 16)
     g.wait_ge(S.snt, sent)
     g.wait_ge(S.st, 16 * (NBD + NR))

from concourse.bass import DstId, RemoteDMATransfer
from concourse.mybir import AluOpType

NB, TK = 16, 128
NSIM = 256
RB = 2
PAIRS = [2, 6]
UNITS = []
_b = 0
for _p in PAIRS:
    UNITS.append((_b, _p // 2))
    UNITS.append((_b + _p // 2, _p // 2))
    _b += _p
ND = len(UNITS)
NBD = _b
for _j in range(4):
    UNITS.append((_b, RB))
    _b += RB
NU = len(UNITS)
PREP = ["T1", "T0", "C0", "C1", "T2", "C2"]
_ACT = ("sbuf", [128, NB * TK], "bfloat16")

SCRATCH = {
    "w": ("sbuf", [128, 256], "bfloat16"),
    "xin": _ACT,
    "h": _ACT,
    "zero": ("sbuf", [128, 512], "float32"),
    "w0r": ("sbuf", [128, 128], "bfloat16"),
    "w1r": ("sbuf", [128, 256], "bfloat16"),
    "w2r": ("sbuf", [128, 256], "bfloat16"),
    "w3r": ("sbuf", [128, 256], "bfloat16"),
    "idz": ("sbuf", [128, 129], "bfloat16"),
    "idd": ("dram", [129, 128], "bfloat16"),
    "ident": ("sbuf", [128, 128], "bfloat16"),
    "wt": ("sbuf", [128, 384], "bfloat16"),
    "cc": ("sbuf", [128, 384], "bfloat16"),
    "a1": _ACT, "a2": _ACT, "a3": _ACT, "a4": _ACT, "a5": _ACT, "a6": _ACT, "yo": _ACT,
    "yd": ("dram", [NB - NBD, 128, TK], "bfloat16"),
    "ps": ("psum", [128, 4096], "float32"),
}
SEMAPHORES = (["lw1", "lw2", "zs", "ids", "id1", "id2", "snt", "ws", "wa1", "wa2", "wa3", "st"]
              + ["pm%d" % i for i in range(4)] + ["pv%d" % i for i in range(4)]
              + ["xs%d" % u for u in range(NU)] + ["m%d" % u for u in range(NU)] + ["v%d" % u for u in range(NU)]
              + ["ha%d" % u for u in range(NU)] + ["yk%d" % j for j in range(4)]
              + ["p" + n for n in PREP] + ["q" + n for n in PREP])


def _engines(topo, src, dst):
    m = topo.mask(src, dst)
    return [e for e in range(m.bit_length()) if (m >> e) & 1]


def _bits(es):
    return sum(1 << e for e in es)


def _turns(topo, cores, c):
    near = [d for d in cores if topo.die(d) == topo.die(c)]
    far = [d for d in cores if topo.die(d) != topo.die(c)]
    out = []
    for i in range(max(len(near), len(far))):
        out += near[i:i + 1] + far[i:i + 1]
    return out


def _owners(topo, c, dst):
    chip = [d for d in range(NSIM) if topo.host(d) == topo.host(c) and topo.chip(d) == topo.chip(c) and d != c]
    return _turns(topo, [d for d in chip if topo.may_write(d, dst)], c)


def _cols(u):
    b, n = UNITS[u]
    return b * TK, (b + n) * TK


def rank_program(g, core, T, topo):
    S = T.sem
    r0, r1, r2, r3 = T.cores
    XR = _owners(topo, r0, r3)[:4]
    WR, V2 = _owners(topo, r2, r3)[:2]
    E1 = _owners(topo, r1, XR[0])[:2]
    E3 = _turns(topo, [c for c in range(NSIM) if topo.mates(c, XR[0]) and topo.may_write(c, XR[0])
                       and topo.may_write(r3, c)], r3)[:2]
    NR = len(XR)
    SW = 128 // NR
    te, ve = g.tensor, g.vector

    def send(dst, out_ap, in_ap, sem, es):
        rid, pid = topo.addr(dst, core)
        g.remote_dma(out_ap=out_ap, in_ap=in_ap, remote_sem=sem, local_sem=S.snt, pid=pid, routing_id=rid,
                     dma_engine_mask=_bits(es))
        return len(es)

    def fused(items, es):
        k = len(es) // len(items)
        trs = []
        for i, (d, out_ap, in_ap, sem) in enumerate(items):
            rid, pid = topo.addr(d, core)
            trs.append(RemoteDMATransfer(dst_ids=[DstId(rid=rid, pnc=pid)], dma_engine_mask=_bits(es[i * k:(i + 1) * k]),
                                         remote_sem=sem, src=in_ap, dst=out_ap))
        g.remote_dma_fused(trs, local_sem=S.snt)
        return k * len(items)

    def load_w(qa, qb):
        qa.dma_start(T.w[:, 0:128], T.w1[:, :]).then_inc(S.lw1, 16)
        qb.dma_start(T.w[:, 128:256], T.w2[:, :]).then_inc(S.lw2, 16)

    def same_die(c):
        return [d for d in XR if topo.die(d) == topo.die(c)]

    on8 = 8

    if core == r0:
        load_w(g.sync, g.scalar)
        for u in range(NU):
            b0, n = UNITS[u]
            for b in range(b0, b0 + n):
                q = g.sync if b % 2 == 0 else g.scalar
                q.dma_start(T.xin[:, b * TK:(b + 1) * TK], T.x[b]).then_inc(S["xs%d" % u], 16)
        ve.memset(T.zero[:, :], 0.0).then_inc(S.zs, 1)
        ve.wait_ge(S.zs, 1)
        te.wait_ge(S.lw1, 16)
        for u in range(NU):
            c0, c1 = _cols(u)
            n = c1 - c0
            bk = T.ps[:, (u % 8) * 512:(u % 8) * 512 + n]
            te.wait_ge(S["xs%d" % u], 16 * UNITS[u][1])
            if u >= 8:
                te.wait_ge(S["v%d" % (u - 8)], 1)
            te.matmul(bk, T.w[:, 0:128], T.xin[:, c0:c1], True, True).then_inc(S["m%d" % u], 1)
            ve.wait_ge(S["m%d" % u], 1)
            ve.tensor_tensor(T.h[:, c0:c1], bk, T.zero[:, 0:n], AluOpType.max).then_inc(S["v%d" % u], 1)
        full = _engines(topo, core, XR[0])
        es = full[:on8]
        g.wait_ge(S.lw2, 16)
        sent = fused([(d, T.w0r[:, :], T.w[:, 128:256], S.ws) for d in XR], es)
        for p in range(ND // 2):
            items = []
            for u in (2 * p, 2 * p + 1):
                c0, c1 = _cols(u)
                g.wait_ge(S["v%d" % u], 1)
                items.append((XR[u % NR], T.h[:, c0:c1], T.h[:, c0:c1], S["ha%d" % u]))
            sent += fused(items, es)
        items = []
        for j in range(NR):
            u = ND + j
            c0, c1 = _cols(u)
            g.wait_ge(S["v%d" % u], 1)
            items.append((XR[j], T.h[:, c0:c1], T.h[:, c0:c1], S["ha%d" % u]))
        sent += fused(items, full)
        g.wait_ge(S.snt, sent)
        return

    if core in XR:
        j = XR.index(core)
        es = _engines(topo, core, r3)
        n_full = len(_engines(topo, r0, XR[0]))
        n_e = len(es) // 2
        g.wait_ge(S.ws, on8 // NR)
        sent = send(r3, T.w0r[:, j * SW:(j + 1) * SW], T.w0r[:, j * SW:(j + 1) * SW], S.ws, es)
        for u in range(ND):
            if u % NR != j:
                continue
            c0, c1 = _cols(u)
            g.wait_ge(S["ha%d" % u], on8 // 2)
            sent += send(r3, T.h[:, c0:c1], T.h[:, c0:c1], S["ha%d" % u], es)
        ve.memset(T.zero[:, :], 0.0).then_inc(S.zs, 1)
        ve.wait_ge(S.zs, 1)
        b0 = UNITS[ND + j][0]
        tiles = [(T.w0r[:, :], (S.ws, on8 // NR)), (T.w1r[:, 0:128], (S.wa1, n_e)), (T.w1r[:, 128:256], None),
                 (T.w2r[:, 0:128], (S.wa2, n_e)), (T.w2r[:, 128:256], None),
                 (T.w3r[:, 0:128], (S.wa3, n_e)), (T.w3r[:, 128:256], None)]
        bufs = [T.h, T.a1, T.a2, T.a3, T.a4, T.a5, T.a6, T.yo]
        NT = len(tiles)
        te.wait_ge(S["ha%d" % (ND + j)], n_full // NR)
        for s, (tile, wt) in enumerate(tiles):
            if wt is not None:
                te.wait_ge(wt[0], wt[1])
            for i in range(RB):
                pm, pv = S["pm%d" % i], S["pv%d" % i]
                c0 = (b0 + i) * TK
                bk = T.ps[:, i * 512:i * 512 + TK]
                if s:
                    te.wait_ge(pv, s)
                te.matmul(bk, tile, bufs[s][:, c0:c0 + TK], True, True).then_inc(pm, 1)
                ve.wait_ge(pm, s + 1)
                if s % 2 == 1:
                    ve.tensor_tensor(bufs[s + 1][:, c0:c0 + TK], bk, T.zero[:, 0:TK], AluOpType.max).then_inc(pv, 1)
                else:
                    ve.tensor_copy(bufs[s + 1][:, c0:c0 + TK], bk).then_inc(pv, 1)
        for i in range(RB):
            g.wait_ge(S["pv%d" % i], NT)
        sent += fused([(r3, T.yd[b0 + i - NBD], T.yo[:, (b0 + i) * TK:(b0 + i + 1) * TK], S["yk%d" % j]) for i in range(RB)], es)
        g.wait_ge(S.snt, sent)
        return

    if core == r1:
        load_w(g.sync, g.scalar)
        g.wait_ge(S.lw1, 16)
        g.wait_ge(S.lw2, 16)
        sent = fused([(d, T.w1r[:, :], T.w[:, :], S.wa1) for d in E1], _engines(topo, core, E1[0])[:on8])
        sent += send(r3, T.w1r[:, :], T.w[:, :], S.wa1, _engines(topo, core, r3))
        g.wait_ge(S.snt, sent)
        return

    for ee, buf, sem in ((E1, T.w1r, S.wa1), (E3, T.w3r, S.wa3), ([V2], T.w2r, S.wa2)):
        if core in ee:
            g.wait_ge(sem, on8 // 2)
            mine = same_die(core)
            sent = fused([(d, buf[:, :], buf[:, :], sem) for d in mine], _engines(topo, core, mine[0]))
            g.wait_ge(S.snt, sent)
            return

    if core == r2:
        load_w(g.sync, g.scalar)
        g.wait_ge(S.lw1, 16)
        g.wait_ge(S.lw2, 16)
        sent = fused([(d, T.w2r[:, :], T.w[:, :], S.wa2) for d in (WR, V2)], _engines(topo, core, WR)[:on8])
        mine = same_die(core)
        sent += fused([(d, T.w2r[:, :], T.w[:, :], S.wa2) for d in mine], _engines(topo, core, mine[0]))
        g.wait_ge(S.snt, sent)
        return
    if core == WR:
        g.wait_ge(S.wa2, on8 // 2)
        sent = send(r3, T.w2r[:, :], T.w2r[:, :], S.wa2, _engines(topo, core, r3))
        g.wait_ge(S.snt, sent)
        return

    if core != r3:
        return

    n_off = len(_engines(topo, XR[0], r3))
    load_w(g.scalar, g.scalar)
    g.wait_ge(S.lw1, 16)
    g.wait_ge(S.lw2, 16)
    sent = fused([(d, T.w3r[:, :], T.w[:, :], S.wa3) for d in E3], _engines(topo, core, E3[0])[:on8])
    ve.memset(T.idz[:, :], 0.0).then_inc(S.ids, 1)
    ve.wait_ge(S.ids, 1)
    ve.memset(T.idz[:, 0:1], 1.0).then_inc(S.ids, 1)
    ve.memset(T.zero[:, :], 0.0).then_inc(S.zs, 1)
    ve.wait_ge(S.zs, 1)
    g.sync.wait_ge(S.ids, 2)
    g.sync.dma_start(T.idd[:, :], T.idz[:, :]).then_inc(S.id1, 16)
    g.sync.wait_ge(S.id1, 16)
    g.sync.dma_start(T.ident[:, :], T.idd[0:128, :]).then_inc(S.id2, 16)

    def prep(name, lhsT, rhs, out, waits):
        bk = T.ps[:, (2 + PREP.index(name)) * 512:(2 + PREP.index(name)) * 512 + 128]
        for s, v in waits:
            te.wait_ge(s, v)
        te.matmul(bk, lhsT, rhs, True, True).then_inc(S["p" + name], 1)
        ve.wait_ge(S["p" + name], 1)
        ve.tensor_copy(out, bk).then_inc(S["q" + name], 1)

    prep("T1", T.w1r[:, 128:256], T.ident[:, :], T.wt[:, 128:256], [(S.id2, 16), (S.wa1, len(_engines(topo, r1, r3)))])
    prep("T0", T.w0r[:, :], T.ident[:, :], T.wt[:, 0:128], [(S.ws, NR * n_off)])
    prep("C0", T.wt[:, 0:128], T.w1r[:, 0:128], T.cc[:, 0:128], [(S.qT0, 1)])
    prep("C1", T.wt[:, 128:256], T.w2r[:, 0:128], T.cc[:, 128:256], [(S.wa2, len(_engines(topo, WR, r3))), (S.qT1, 1)])
    prep("T2", T.w2r[:, 128:256], T.ident[:, :], T.wt[:, 256:384], [])

    cnt = [0, 0]
    pm, pv = [S.pm0, S.pm1], [S.pv0, S.pv1]
    lhs = [T.cc[:, 0:128], T.cc[:, 128:256], T.cc[:, 256:384], T.w[:, 128:256]]
    act = [T.h, T.a1, T.a2, T.a3, T.yo]
    ready = [(S.qC0, 1), (S.qC1, 1), (S.qC2, 1), (S.lw2, 16)]
    for p in range(ND // 2):
        for s in range(4):
            if p == 0:
                te.wait_ge(ready[s][0], ready[s][1])
            for i in range(2):
                u = 2 * p + i
                c0, c1 = _cols(u)
                n = c1 - c0
                bk = T.ps[:, i * 512:i * 512 + n]
                if s == 0:
                    te.wait_ge(S["ha%d" % u], n_off)
                if cnt[i]:
                    te.wait_ge(pv[i], cnt[i])
                te.matmul(bk, lhs[s], act[s][:, c0:c1], True, True).then_inc(pm[i], 1)
                cnt[i] += 1
                ve.wait_ge(pm[i], cnt[i])
                if s < 3:
                    ve.tensor_tensor(act[s + 1][:, c0:c1], bk, T.zero[:, 0:n], AluOpType.max).then_inc(pv[i], 1)
                else:
                    ve.tensor_copy(T.yo[:, c0:c1], bk).then_inc(pv[i], 1)
                    b0, nb = UNITS[u]
                    g.sync.wait_ge(pv[i], cnt[i])
                    for b in range(b0, b0 + nb):
                        g.sync.dma_start(T.y[b], T.yo[:, b * TK:(b + 1) * TK]).then_inc(S.st, 16)
            if p == 0 and s == 0:
                prep("C2", T.wt[:, 256:384], T.w[:, 0:128], T.cc[:, 256:384], [(S.qT2, 1), (S.lw1, 16)])
    for j in range(NR):
        b0 = UNITS[ND + j][0]
        g.scalar.wait_ge(S["yk%d" % j], (n_off // RB) * RB)
        g.scalar.dma_start(T.y[b0:b0 + RB], T.yd[b0 - NBD:b0 - NBD + RB]).then_inc(S.st, 16)
    g.wait_ge(S.snt, sent)
    g.wait_ge(S.st, 16 * (NBD + NR))
